import numpy as np
import ml_dtypes


def mxq(x, axis, fmt="e4m3"):
    dtype, down = {"e4m3": (ml_dtypes.float8_e4m3fn, 7), "e5m2": (ml_dtypes.float8_e5m2, 14)}[fmt]
    v = np.moveaxis(np.asarray(x, np.float32).astype(ml_dtypes.bfloat16).astype(np.float64), axis, -1)
    blocks = v.reshape(v.shape[:-1] + (-1, 32))
    amax = np.abs(blocks).max(-1, keepdims=True)
    byte = np.maximum(np.where(amax > 0, np.frexp(amax)[1] - 1 + 127, 0) - down, 1)
    scale = np.exp2(byte - 127.0)
    codes = (blocks / scale).astype(np.float32).astype(dtype).astype(np.float64)
    return np.moveaxis((codes * scale).reshape(v.shape), -1, axis)


WIDE = False


def mx_kscale(k):
    if not WIDE:
        return np.ones(k)
    levels = np.array([10, -10, 5, -5, 0])
    if k % 512:
        return np.exp2(np.random.permutation(np.resize(levels, k // 32))).repeat(32)
    a = np.empty((k // 512, 16))
    for p in range(k // 512):
        a[p, :8] = np.random.permutation(np.resize(levels, 8))
        for g in range(8):
            far = levels[np.abs(levels - a[p, g]) >= 10]
            a[p, g + 8] = far[np.random.randint(len(far))]
    return np.exp2(a.ravel()).repeat(32)


def f64(x):
    return np.asarray(x).astype(np.float64)


def striped(idx):
    return np.tile(idx.reshape(-1, 16).T, (8, 1)).astype(np.uint16)


def unstriped(offs):
    return offs[:16].T.reshape(-1).astype(np.int64)


E2M1 = np.array([0.0, 0.5, 1.0, 1.5, 2.0, 3.0, 4.0, 6.0, -0.0, -0.5, -1.0, -1.5, -2.0, -3.0, -4.0, -6.0])


def pack_weight(w, fmt):
    k, n = w.shape
    w = f64(np.asarray(w, np.float32).astype(ml_dtypes.bfloat16)).reshape(k // 32, 32, n)
    amax = np.abs(w).max(1)
    if fmt == "e4m3":
        byte = np.frexp(amax)[1] - 1 + 127 - 7
    else:
        mant, ex = np.frexp(amax / 6.0)
        byte = np.where(mant > 0.5, ex, ex - 1) + 127
    byte = np.clip(np.where(amax > 0, byte, 1), 1, 254)
    scaled = (w * np.exp2(127.0 - byte)[:, None, :]).reshape(k, n).astype(np.float32)
    by_word = np.ascontiguousarray(scaled.reshape(k // 512, 128, 4, n).transpose(0, 1, 3, 2))
    if fmt == "e4m3":
        words = by_word.astype(ml_dtypes.float8_e4m3fn).view(np.uint8)
    else:
        c = by_word.astype(ml_dtypes.float4_e2m1fn).view(np.uint8) & 0xF
        words = (c[..., 0::2] | (c[..., 1::2] << 4)).reshape(k // 512, 128, 2 * n)
    return np.ascontiguousarray(words), np.ascontiguousarray(byte.astype(np.uint8).reshape(k // 512, 16, n))


def unpack_weight(words, scales, fmt):
    g, _, n = scales.shape
    words = np.ascontiguousarray(words).reshape(g, 128, n, -1)
    if fmt == "e4m3":
        vals = words.view(ml_dtypes.float8_e4m3fn).astype(np.float64)
    else:
        nib = np.empty((g, 128, n, 4), np.uint8)
        nib[..., 0::2] = words & 0xF
        nib[..., 1::2] = words >> 4
        vals = E2M1[nib]
    vals = vals * np.repeat(np.exp2(scales.astype(np.float64) - 127.0), 8, axis=1)[..., None]
    return vals.transpose(0, 1, 3, 2).reshape(g * 512, n)


def gelu(v):
    return 0.5 * v * (1.0 + np.tanh(np.sqrt(2.0 / np.pi) * (v + 0.044715 * v**3)))


K, T, S, H, N = 1024, 4096, 512, 512, 768

def setup_inputs():
    n = np.random.standard_normal
    s = mx_kscale(K)[:, None]
    u = mx_kscale(H)[:, None]
    tab_words, tab_scales = pack_weight(n((K, T)) * s, "e4m3")
    w1_words, w1_scales = pack_weight(n((K, H)) / np.sqrt(K) / s, "e2m1")
    w2 = (0.56 * n((K, H)) / np.sqrt(K) / s).astype(np.float32)
    w3 = (0.5 * n((K, H)) / np.sqrt(K) / s).astype(np.float32)
    gain = (np.exp(0.3 * n(H)) * u[:, 0]).astype(np.float32)
    w4_words, w4_scales = pack_weight(n((H, N)) / np.sqrt(H) / u, "e4m3")
    w5 = (n((K, N)) / np.sqrt(K) / s).astype(np.float32)
    return {"tab_words": tab_words, "tab_scales": tab_scales,
            "offs": striped(np.random.permutation(T)[:S]),
            "offs2": striped(np.random.permutation(T)[:S]),
            "offs3": striped(np.random.permutation(T)[:S]),
            "w1_words": w1_words, "w1_scales": w1_scales,
            "w2": w2, "w3": w3, "gain": gain,
            "w4_words": w4_words, "w4_scales": w4_scales, "w5": w5}

def reference(tab_words, tab_scales, offs, offs2, offs3, w1_words, w1_scales,
              w2, w3, gain, w4_words, w4_scales, w5):
    TW = unpack_weight(tab_words, tab_scales, "e4m3")
    v = TW[:, unstriped(offs)]
    v2 = TW[:, unstriped(offs2)]
    v3 = TW[:, unstriped(offs3)]
    helper = unpack_weight(w1_words, w1_scales, "e2m1").T @ v
    request = mxq(f64(w2), 0, "e4m3").T @ v2
    district = mxq(f64(w3), 0, "e4m3").T @ v3
    mixed = np.tanh(helper) + np.sin(request) + np.abs(district)
    h = f64(gain)[:, None] * mixed
    hq = mxq(h, 0, "e4m3")
    y = unpack_weight(w4_words, w4_scales, "e4m3").T @ hq
    d = mxq(f64(w5), 0, "e4m3").T @ v3
    return y * d

@@ -1,0 +1,262 @@
+import math
+from contextlib import ExitStack
+
+import concourse.mybir as mybir
+from concourse.masks import make_identity
+
+K, T, S, H, N = 1024, 4096, 512, 512, 768
+FLOPS = 2 * S * (3 * K * H + H * N + K * N)
+
+F32 = mybir.dt.float32
+BF16 = mybir.dt.bfloat16
+I32 = mybir.dt.int32
+U32 = mybir.dt.uint32
+U16 = mybir.dt.uint16
+U8 = mybir.dt.uint8
+FP8X4 = mybir.dt.float8_e4m3fn_x4
+FP4X4 = mybir.dt.float4_e2m1fn_x4
+ACT = mybir.ActivationFunctionType
+ALU = mybir.AluOpType
+
+P = 128
+PACK = 4
+K_PASS = P * PACK
+PASSES = K // K_PASS
+QUADS = 4
+PART = 256
+J_TILES = S // P
+
+
+def tile_list_timebank_offer_features_kernel(
+    tc, tab_words, tab_scales, offs, offs2, offs3, w1_words, w1_scales, w2, w3, gain, w4_words, w4_scales, w5, out
+):
+    nc = tc.nc
+    with ExitStack() as ctx:
+        keep = ctx.enter_context(tc.tile_pool(name="keep", bufs=1))
+        psum = ctx.enter_context(tc.psum_pool(name="psum", bufs=1))
+
+        def kept(shape, dtype, name, tag=None):
+            return keep.tile(shape, dtype, name=name, tag=tag or name, align_bytes=64)
+
+        lists = [keep.tile([P, S // 16], U16, name=f"list{u}") for u in range(3)]
+        tab_w = [kept([P, T], I32, f"tab_w{a}") for a in range(PASSES)]
+        tab_s = kept([P, T], U8, "tab_s")
+        w1_w = kept([P, PASSES, 2 * H], U8, "w1_w")
+        w1_s = kept([P, PASSES, H], U8, "w1_s")
+        w4_w = kept([P, N], I32, "w4_w")
+        w4_s = kept([P, N], U8, "w4_s")
+        moved_s = kept([P, S], U8, "moved_s")
+        gains = kept([P, PACK], F32, "gains")
+        ident = kept([P, P], F32, "ident")
+        one = kept([P, 1], F32, "one")
+        quarter_pi = kept([P, 1], F32, "quarter_pi")
+
+        nc.vector.memset(tab_s[:].bitcast(I32), 0)
+        nc.vector.memset(one[:], 1.0)
+        nc.vector.tensor_scalar(out=quarter_pi[:], in0=one[:], scalar1=math.pi / 4.0, scalar2=None, op0=ALU.mult)
+        nc.gpsimd.memset(w1_s[:].rearrange("p a c -> p (a c)").bitcast(I32), 0)
+        nc.gpsimd.memset(moved_s[:].bitcast(I32), 0)
+        nc.gpsimd.memset(w4_s[:].bitcast(I32), 0)
+
+        def load_rows(w, a, c0, c1, name):
+            raw = kept([P, PACK, c1 - c0], F32, name)
+            rows = w[a * K_PASS : (a + 1) * K_PASS, c0:c1]
+            nc.sync.dma_start(out=raw[:], in_=rows.rearrange("(p i) c -> p i c", i=PACK))
+            return raw
+
+        def load_table(a):
+            nc.sync.dma_start(out=tab_w[a][:], in_=tab_words[a].rearrange("p t i -> p (t i)").bitcast(I32))
+
+        for tile, src in zip(lists, (offs, offs2, offs3)):
+            nc.sync.dma_start(tile[:], src)
+        for q in range(QUADS):
+            nc.sync.dma_start(
+                out=tab_s[32 * q : 32 * q + 4 * PASSES, :].bitcast(I32),
+                in_=tab_scales[:, 4 * q : 4 * q + 4, :].bitcast(I32),
+            )
+        load_table(0)
+        for q in range(QUADS):
+            nc.sync.dma_start(
+                out=w1_s[32 * q : 32 * q + 4, :, :].bitcast(I32),
+                in_=w1_scales[:, 4 * q : 4 * q + 4, :].rearrange("a r c -> r a c").bitcast(I32),
+            )
+        nc.sync.dma_start(out=w1_w[:].bitcast(I32), in_=w1_words.rearrange("a p c -> p a c").bitcast(I32))
+        load_table(1)
+        w2_raw = [load_rows(w2, a, 0, H, f"w2_raw{a}") for a in range(PASSES)]
+        w3_raw = [load_rows(w3, a, 0, H, f"w3_raw{a}") for a in range(PASSES)]
+        nc.sync.dma_start(out=gains[:], in_=gain.rearrange("(p i) -> p i", i=PACK))
+        w5_raw0 = load_rows(w5, 0, 0, N, "w5_raw0")
+        w5_raw1a = load_rows(w5, 1, 0, 2 * PART, "w5_raw1a")
+        w5_raw1b = load_rows(w5, 1, 2 * PART, N, "w5_raw1b")
+        for q in range(QUADS):
+            nc.sync.dma_start(
+                out=w4_s[32 * q : 32 * q + 4, :].bitcast(I32), in_=w4_scales[0, 4 * q : 4 * q + 4, :].bitcast(I32)
+            )
+        nc.sync.dma_start(out=w4_w[:], in_=w4_words[0].rearrange("p c i -> p (c i)").bitcast(I32))
+        make_identity(nc, ident[:])
+
+        got_s = [kept([P, S], U8, f"got_s{u}") for u in range(3)]
+        got_w = [[None] * PASSES for u in range(3)]
+
+        def gather_words(u, a, tag=None):
+            got_w[u][a] = kept([P, S], U32, f"got_w{u}{a}", tag)
+            nc.vector.tensor_copy(got_w[u][a][:], tab_w[a][:].bitcast(U32).indirect(lists[u][:]))
+
+        for u in range(3):
+            nc.vector.tensor_copy(got_s[u][:], tab_s[:].indirect(lists[u][:]))
+        nc.scalar.dma_start(out=moved_s[0:112, :].bitcast(I32), in_=got_s[0][4:116, :].bitcast(I32))
+        for u in range(3):
+            gather_words(u, 0)
+        gather_words(0, 1)
+        gather_words(1, 1)
+
+        seen = {}
+
+        def round_part(copy, raw, c0, name, tag=None):
+            grouped = kept([P, PART, PACK], BF16, name, tag)
+            seen[name] = grouped
+            copy(
+                out=grouped[:].rearrange("p (c e) i -> p c i e", e=4),
+                in_=raw[:, :, c0 : c0 + PART].rearrange("p i (c e) -> p c i e", e=4),
+            )
+            return grouped
+
+        def quantise(grouped, dest, d0):
+            width = grouped.shape[1]
+            nc.vector.quantize_mx(
+                out=dest[0][:, d0 : d0 + width].bitcast(FP8X4),
+                scales=dest[1][:, d0 : d0 + width],
+                in_=grouped[:].rearrange("p c i -> p (c i)"),
+            )
+
+        def quantised(width, name):
+            return kept([P, width], U32, name + "_w"), kept([P, width], U8, name + "_s")
+
+        def prepare(copies, raw, dest, name):
+            groups = [round_part(cp, raw, g * PART, f"{name}_{g}") for g, cp in enumerate(copies)]
+            for g, grouped in enumerate(groups):
+                quantise(grouped, dest, g * PART)
+
+        on_vector = nc.vector.tensor_copy
+        on_scalar = nc.scalar.copy
+
+        def first_product(u, planes, moving, half):
+            banks = [psum.tile([P, H], F32, name="bank", tag=f"{half}{jt}") for jt in range(J_TILES)]
+            for a in range(PASSES):
+                for jt in range(J_TILES):
+                    cols = slice(jt * P, (jt + 1) * P)
+                    nc.tensor.matmul_mx(
+                        out=banks[jt][:],
+                        lhsT=got_w[u][a][:, cols].bitcast(FP8X4),
+                        lhsT_scale=planes[a][:, cols],
+                        rhs=moving[a][0],
+                        rhs_scale=moving[a][1],
+                        start=(a == 0),
+                        stop=(a == PASSES - 1),
+                    )
+            return [bank[:].rearrange("j (p i) -> j i p", i=PACK) for bank in banks]
+
+        def add_turned(jt, term, first, last):
+            for i in range(PACK):
+                nc.tensor.matmul(
+                    out=sums[jt][:, i, :],
+                    lhsT=term[:, i, :],
+                    rhs=ident[:],
+                    is_transpose=True,
+                    start=(first and i == 0),
+                    stop=(last and i == PACK - 1),
+                )
+
+        def through(func, sources, name, **how):
+            terms = [kept([P, PACK, P], F32, f"{name}{jt}") for jt in range(J_TILES)]
+            for term, source in zip(terms, sources):
+                nc.scalar.activation(out=term[:], in_=source, func=func, **how)
+            return terms
+
+        def planes_of(u):
+            return [got_s[u][4 * a : P, :] for a in range(PASSES)]
+
+        def moving_of(q):
+            return [(q[a][0][:].bitcast(FP8X4), q[a][1][:]) for a in range(PASSES)]
+
+        w1_moving = [(w1_w[:, a, :].bitcast(FP4X4), w1_s[:, a, :]) for a in range(PASSES)]
+        tanhs = through(ACT.Tanh, first_product(0, [got_s[0], moved_s], w1_moving, "low"), "tanh")
+
+        w2_q = [quantised(H, f"w2_q{a}") for a in range(PASSES)]
+        prepare([on_vector, on_vector], w2_raw[0], w2_q[0], "w2a")
+        prepare([on_vector, on_vector], w2_raw[1], w2_q[1], "w2b")
+
+        request = first_product(1, planes_of(1), moving_of(w2_q), "high")
+        halves = through(ACT.Sin, request, "half", scale=0.5, bias=quarter_pi[:])
+        sums = [psum.tile([P, PACK, P], F32, name="sum", tag=f"high{jt}") for jt in range(J_TILES)]
+        for jt in range(J_TILES):
+            add_turned(jt, tanhs[jt], True, False)
+        squares = through(ACT.Square, [t[:] for t in halves], "square", scale=math.sqrt(2.0))
+
+        gather_words(2, 1, "got_w11")
+        w3_q = [quantised(H, f"w3_q{a}") for a in range(PASSES)]
+        for a in range(PASSES):
+            prepare([on_vector, on_vector], w3_raw[a], w3_q[a], f"w3{a}")
+
+        sizes = through(ACT.Abs, first_product(2, planes_of(2), moving_of(w3_q), "low"), "size")
+        for jt in range(J_TILES):
+            add_turned(jt, squares[jt], False, False)
+
+        w5_q = [quantised(N, f"w5_q{a}") for a in range(PASSES)]
+        prepare([on_vector, on_vector], w5_raw0, w5_q[0], "w5a")
+
+        h_grouped = kept([P, S, PACK], BF16, "h_grouped")
+        for jt in range(J_TILES):
+            add_turned(jt, sizes[jt], False, True)
+            nc.vector.scalar_tensor_tensor(
+                out=h_grouped[:, jt * P : (jt + 1) * P, :],
+                in0=sums[jt][:].rearrange("p i j -> p j i"),
+                scalar=1.0,
+                in1=gains[:].unsqueeze(1).to_broadcast([P, P, PACK]),
+                op0=ALU.subtract,
+                op1=ALU.mult,
+            )
+        late = [
+            (round_part(on_scalar, w5_raw0, 2 * PART, "w5a_2", "size0"), 0, 2 * PART),
+            (round_part(on_scalar, w5_raw1a, 0, "w5b_0", "size1"), 1, 0),
+            (round_part(on_scalar, w5_raw1a, PART, "w5b_1", "size2"), 1, PART),
+            (round_part(on_scalar, w5_raw1b, 0, "w5b_2", "size3"), 1, 2 * PART),
+        ]
+        h_q = quantised(S, "h_q")
+        quantise(h_grouped, h_q, 0)
+        for grouped, a, d0 in late:
+            quantise(grouped, w5_q[a], d0)
+
+        ys = []
+        for nt in range(N // P):
+            cols = slice(nt * P, (nt + 1) * P)
+            y_bank = psum.tile([P, S], F32, name="y_bank", tag=f"low{nt % J_TILES}")
+            nc.tensor.matmul_mx(
+                out=y_bank[:],
+                lhsT=w4_w[:, cols].bitcast(FP8X4),
+                lhsT_scale=w4_s[:, cols],
+                rhs=h_q[0][:].bitcast(FP8X4),
+                rhs_scale=h_q[1][:],
+                start=True,
+                stop=True,
+            )
+            y = kept([P, S], F32, f"y{nt}")
+            nc.scalar.copy(out=y[:], in_=y_bank[:])
+            ys.append(y)
+        for nt in range(N // P):
+            cols = slice(nt * P, (nt + 1) * P)
+            d_bank = psum.tile([P, PACK, P], F32, name="d_bank", tag=f"high{nt % J_TILES}")
+            d_flat = d_bank[:].rearrange("p i j -> p (i j)")
+            for a in range(PASSES):
+                nc.tensor.matmul_mx(
+                    out=d_flat,
+                    lhsT=w5_q[a][0][:, cols].bitcast(FP8X4),
+                    lhsT_scale=w5_q[a][1][:, cols],
+                    rhs=got_w[2][a][:].bitcast(FP8X4),
+                    rhs_scale=got_s[2][4 * a : P, :],
+                    start=(a == 0),
+                    stop=(a == PASSES - 1),
+                )
+            res = kept([P, S], F32, f"res{nt}")
+            nc.vector.tensor_tensor(out=res[:], in0=d_flat, in1=ys[nt][:], op=ALU.mult)
+            nc.sync.dma_start(out=out[cols, :], in_=res[:])

@@ -23,8 +23,14 @@ PACK = 4
 K_PASS = P * PACK
 PASSES = K // K_PASS
 QUADS = 4
+QUAD = P // QUADS
+ROWS = 4
+PLANE_SPAN = (QUADS - 1) * QUAD + ROWS
+LIST_GROUP = 16
 PART = 256
+RUN = 4
 J_TILES = S // P
+HELPER, REQUEST, DISTRICT = 0, 1, 2
 
 
 def tile_list_timebank_offer_features_kernel(
@@ -38,7 +44,7 @@ def tile_list_timebank_offer_features_kernel(
         def kept(shape, dtype, name, tag=None):
             return keep.tile(shape, dtype, name=name, tag=tag or name, align_bytes=64)
 
-        lists = [keep.tile([P, S // 16], U16, name=f"list{u}") for u in range(3)]
+        lists = [keep.tile([P, S // LIST_GROUP], U16, name=f"list{u}") for u in (HELPER, REQUEST, DISTRICT)]
         tab_w = [kept([P, T], I32, f"tab_w{a}") for a in range(PASSES)]
         tab_s = kept([P, T], U8, "tab_s")
         w1_w = kept([P, PASSES, 2 * H], U8, "w1_w")
@@ -67,18 +73,18 @@ def tile_list_timebank_offer_features_kernel(
         def load_table(a):
             nc.sync.dma_start(out=tab_w[a][:], in_=tab_words[a].rearrange("p t i -> p (t i)").bitcast(I32))
 
-        for tile, src in zip(lists, (offs, offs2, offs3)):
-            nc.sync.dma_start(tile[:], src)
-        for q in range(QUADS):
+        for list_tile, list_input in zip(lists, (offs, offs2, offs3)):
+            nc.sync.dma_start(list_tile[:], list_input)
+        for quad in range(QUADS):
             nc.sync.dma_start(
-                out=tab_s[32 * q : 32 * q + 4 * PASSES, :].bitcast(I32),
-                in_=tab_scales[:, 4 * q : 4 * q + 4, :].bitcast(I32),
+                out=tab_s[QUAD * quad : QUAD * quad + ROWS * PASSES, :].bitcast(I32),
+                in_=tab_scales[:, ROWS * quad : ROWS * (quad + 1), :].bitcast(I32),
             )
         load_table(0)
-        for q in range(QUADS):
+        for quad in range(QUADS):
             nc.sync.dma_start(
-                out=w1_s[32 * q : 32 * q + 4, :, :].bitcast(I32),
-                in_=w1_scales[:, 4 * q : 4 * q + 4, :].rearrange("a r c -> r a c").bitcast(I32),
+                out=w1_s[QUAD * quad : QUAD * quad + ROWS, :, :].bitcast(I32),
+                in_=w1_scales[:, ROWS * quad : ROWS * (quad + 1), :].rearrange("a s c -> s a c").bitcast(I32),
             )
         nc.sync.dma_start(out=w1_w[:].bitcast(I32), in_=w1_words.rearrange("a p c -> p a c").bitcast(I32))
         load_table(1)
@@ -88,57 +94,54 @@ def tile_list_timebank_offer_features_kernel(
         w5_raw0 = load_rows(w5, 0, 0, N, "w5_raw0")
         w5_raw1a = load_rows(w5, 1, 0, 2 * PART, "w5_raw1a")
         w5_raw1b = load_rows(w5, 1, 2 * PART, N, "w5_raw1b")
-        for q in range(QUADS):
+        for quad in range(QUADS):
             nc.sync.dma_start(
-                out=w4_s[32 * q : 32 * q + 4, :].bitcast(I32), in_=w4_scales[0, 4 * q : 4 * q + 4, :].bitcast(I32)
+                out=w4_s[QUAD * quad : QUAD * quad + ROWS, :].bitcast(I32),
+                in_=w4_scales[0, ROWS * quad : ROWS * (quad + 1), :].bitcast(I32),
             )
         nc.sync.dma_start(out=w4_w[:], in_=w4_words[0].rearrange("p c i -> p (c i)").bitcast(I32))
         make_identity(nc, ident[:])
 
-        got_s = [kept([P, S], U8, f"got_s{u}") for u in range(3)]
-        got_w = [[None] * PASSES for u in range(3)]
+        got_s = [kept([P, S], U8, f"got_s{u}") for u in (HELPER, REQUEST, DISTRICT)]
+        got_w = [[None] * PASSES for u in (HELPER, REQUEST, DISTRICT)]
 
         def gather_words(u, a, tag=None):
             got_w[u][a] = kept([P, S], U32, f"got_w{u}{a}", tag)
             nc.vector.tensor_copy(got_w[u][a][:], tab_w[a][:].bitcast(U32).indirect(lists[u][:]))
 
-        for u in range(3):
+        for u in (HELPER, REQUEST, DISTRICT):
             nc.vector.tensor_copy(got_s[u][:], tab_s[:].indirect(lists[u][:]))
-        nc.scalar.dma_start(out=moved_s[0:112, :].bitcast(I32), in_=got_s[0][4:116, :].bitcast(I32))
-        for u in range(3):
+        nc.scalar.dma_start(
+            out=moved_s[0:PLANE_SPAN, :].bitcast(I32), in_=got_s[HELPER][ROWS : ROWS + PLANE_SPAN, :].bitcast(I32)
+        )
+        for u in (HELPER, REQUEST, DISTRICT):
             gather_words(u, 0)
-        gather_words(0, 1)
-        gather_words(1, 1)
-
-        seen = {}
+        gather_words(HELPER, 1)
+        gather_words(REQUEST, 1)
 
         def round_part(copy, raw, c0, name, tag=None):
             grouped = kept([P, PART, PACK], BF16, name, tag)
-            seen[name] = grouped
             copy(
-                out=grouped[:].rearrange("p (c e) i -> p c i e", e=4),
-                in_=raw[:, :, c0 : c0 + PART].rearrange("p i (c e) -> p c i e", e=4),
+                out=grouped[:].rearrange("p (c e) i -> p c i e", e=RUN),
+                in_=raw[:, :, c0 : c0 + PART].rearrange("p i (c e) -> p c i e", e=RUN),
             )
             return grouped
 
-        def quantise(grouped, dest, d0):
+        def quantise(grouped, operand, c0):
             width = grouped.shape[1]
             nc.vector.quantize_mx(
-                out=dest[0][:, d0 : d0 + width].bitcast(FP8X4),
-                scales=dest[1][:, d0 : d0 + width],
+                out=operand[0][:, c0 : c0 + width].bitcast(FP8X4),
+                scales=operand[1][:, c0 : c0 + width],
                 in_=grouped[:].rearrange("p c i -> p (c i)"),
             )
 
-        def quantised(width, name):
+        def new_operand(width, name):
             return kept([P, width], U32, name + "_w"), kept([P, width], U8, name + "_s")
 
-        def prepare(copies, raw, dest, name):
-            groups = [round_part(cp, raw, g * PART, f"{name}_{g}") for g, cp in enumerate(copies)]
+        def two_parts_on_vector(raw, operand, name):
+            groups = [round_part(nc.vector.tensor_copy, raw, g * PART, f"{name}_{g}") for g in range(2)]
             for g, grouped in enumerate(groups):
-                quantise(grouped, dest, g * PART)
-
-        on_vector = nc.vector.tensor_copy
-        on_scalar = nc.scalar.copy
+                quantise(grouped, operand, g * PART)
 
         def first_product(u, planes, moving, half):
             banks = [psum.tile([P, H], F32, name="bank", tag=f"{half}{jt}") for jt in range(J_TILES)]
@@ -174,36 +177,36 @@ def tile_list_timebank_offer_features_kernel(
             return terms
 
         def planes_of(u):
-            return [got_s[u][4 * a : P, :] for a in range(PASSES)]
+            return [got_s[u][ROWS * a : P, :] for a in range(PASSES)]
 
-        def moving_of(q):
-            return [(q[a][0][:].bitcast(FP8X4), q[a][1][:]) for a in range(PASSES)]
+        def moving_of(operands):
+            return [(words[:].bitcast(FP8X4), scales[:]) for words, scales in operands]
 
         w1_moving = [(w1_w[:, a, :].bitcast(FP4X4), w1_s[:, a, :]) for a in range(PASSES)]
-        tanhs = through(ACT.Tanh, first_product(0, [got_s[0], moved_s], w1_moving, "low"), "tanh")
+        tanhs = through(ACT.Tanh, first_product(HELPER, [got_s[HELPER], moved_s], w1_moving, "low"), "tanh")
 
-        w2_q = [quantised(H, f"w2_q{a}") for a in range(PASSES)]
-        prepare([on_vector, on_vector], w2_raw[0], w2_q[0], "w2a")
-        prepare([on_vector, on_vector], w2_raw[1], w2_q[1], "w2b")
+        w2_q = [new_operand(H, f"w2_q{a}") for a in range(PASSES)]
+        for a in range(PASSES):
+            two_parts_on_vector(w2_raw[a], w2_q[a], f"w2_{a}")
 
-        request = first_product(1, planes_of(1), moving_of(w2_q), "high")
-        halves = through(ACT.Sin, request, "half", scale=0.5, bias=quarter_pi[:])
+        request = first_product(REQUEST, planes_of(REQUEST), moving_of(w2_q), "high")
+        sines = through(ACT.Sin, request, "sine", scale=0.5, bias=quarter_pi[:])
         sums = [psum.tile([P, PACK, P], F32, name="sum", tag=f"high{jt}") for jt in range(J_TILES)]
         for jt in range(J_TILES):
             add_turned(jt, tanhs[jt], True, False)
-        squares = through(ACT.Square, [t[:] for t in halves], "square", scale=math.sqrt(2.0))
+        squares = through(ACT.Square, [sine[:] for sine in sines], "square", scale=math.sqrt(2.0))
 
-        gather_words(2, 1, "got_w11")
-        w3_q = [quantised(H, f"w3_q{a}") for a in range(PASSES)]
+        gather_words(DISTRICT, 1, f"got_w{REQUEST}1")
+        w3_q = [new_operand(H, f"w3_q{a}") for a in range(PASSES)]
         for a in range(PASSES):
-            prepare([on_vector, on_vector], w3_raw[a], w3_q[a], f"w3{a}")
+            two_parts_on_vector(w3_raw[a], w3_q[a], f"w3_{a}")
 
-        sizes = through(ACT.Abs, first_product(2, planes_of(2), moving_of(w3_q), "low"), "size")
+        sizes = through(ACT.Abs, first_product(DISTRICT, planes_of(DISTRICT), moving_of(w3_q), "low"), "size")
         for jt in range(J_TILES):
             add_turned(jt, squares[jt], False, False)
 
-        w5_q = [quantised(N, f"w5_q{a}") for a in range(PASSES)]
-        prepare([on_vector, on_vector], w5_raw0, w5_q[0], "w5a")
+        w5_q = [new_operand(N, f"w5_q{a}") for a in range(PASSES)]
+        two_parts_on_vector(w5_raw0, w5_q[0], "w5_0")
 
         h_grouped = kept([P, S, PACK], BF16, "h_grouped")
         for jt in range(J_TILES):
@@ -216,16 +219,19 @@ def tile_list_timebank_offer_features_kernel(
                 op0=ALU.subtract,
                 op1=ALU.mult,
             )
-        late = [
-            (round_part(on_scalar, w5_raw0, 2 * PART, "w5a_2", "size0"), 0, 2 * PART),
-            (round_part(on_scalar, w5_raw1a, 0, "w5b_0", "size1"), 1, 0),
-            (round_part(on_scalar, w5_raw1a, PART, "w5b_1", "size2"), 1, PART),
-            (round_part(on_scalar, w5_raw1b, 0, "w5b_2", "size3"), 1, 2 * PART),
+        scalar_parts = [
+            (w5_raw0, 2 * PART, 0, 2 * PART),
+            (w5_raw1a, 0, 1, 0),
+            (w5_raw1a, PART, 1, PART),
+            (w5_raw1b, 0, 1, 2 * PART),
         ]
-        h_q = quantised(S, "h_q")
+        scalar_groups = [
+            round_part(nc.scalar.copy, part[0], part[1], f"w5_late{g}", f"size{g}") for g, part in enumerate(scalar_parts)
+        ]
+        h_q = new_operand(S, "h_q")
         quantise(h_grouped, h_q, 0)
-        for grouped, a, d0 in late:
-            quantise(grouped, w5_q[a], d0)
+        for grouped, part in zip(scalar_groups, scalar_parts):
+            quantise(grouped, w5_q[part[2]], part[3])
 
         ys = []
         for nt in range(N // P):
@@ -245,18 +251,17 @@ def tile_list_timebank_offer_features_kernel(
             ys.append(y)
         for nt in range(N // P):
             cols = slice(nt * P, (nt + 1) * P)
-            d_bank = psum.tile([P, PACK, P], F32, name="d_bank", tag=f"high{nt % J_TILES}")
-            d_flat = d_bank[:].rearrange("p i j -> p (i j)")
+            d_bank = psum.tile([P, S], F32, name="d_bank", tag=f"high{nt % J_TILES}")
             for a in range(PASSES):
                 nc.tensor.matmul_mx(
-                    out=d_flat,
+                    out=d_bank[:],
                     lhsT=w5_q[a][0][:, cols].bitcast(FP8X4),
                     lhsT_scale=w5_q[a][1][:, cols],
-                    rhs=got_w[2][a][:].bitcast(FP8X4),
-                    rhs_scale=got_s[2][4 * a : P, :],
+                    rhs=got_w[DISTRICT][a][:].bitcast(FP8X4),
+                    rhs_scale=planes_of(DISTRICT)[a],
                     start=(a == 0),
                     stop=(a == PASSES - 1),
                 )
-            res = kept([P, S], F32, f"res{nt}")
-            nc.vector.tensor_tensor(out=res[:], in0=d_flat, in1=ys[nt][:], op=ALU.mult)
-            nc.sync.dma_start(out=out[cols, :], in_=res[:])
+            result = kept([P, S], F32, f"result{nt}")
+            nc.vector.tensor_tensor(out=result[:], in0=d_bank[:], in1=ys[nt][:], op=ALU.mult)
+            nc.sync.dma_start(out=out[cols, :], in_=result[:])

import math
from contextlib import ExitStack

import concourse.mybir as mybir
from concourse.masks import make_identity

K, T, S, H, N = 1024, 4096, 512, 512, 768
FLOPS = 2 * S * (3 * K * H + H * N + K * N)

F32 = mybir.dt.float32
BF16 = mybir.dt.bfloat16
I32 = mybir.dt.int32
U32 = mybir.dt.uint32
U16 = mybir.dt.uint16
U8 = mybir.dt.uint8
FP8X4 = mybir.dt.float8_e4m3fn_x4
FP4X4 = mybir.dt.float4_e2m1fn_x4
ACT = mybir.ActivationFunctionType
ALU = mybir.AluOpType

P = 128
PACK = 4
K_PASS = P * PACK
PASSES = K // K_PASS
QUADS = 4
QUAD = P // QUADS
ROWS = 4
PLANE_SPAN = (QUADS - 1) * QUAD + ROWS
LIST_GROUP = 16
PART = 256
RUN = 4
J_TILES = S // P
HELPER, REQUEST, DISTRICT = 0, 1, 2


def tile_list_timebank_offer_features_kernel(
    tc, tab_words, tab_scales, offs, offs2, offs3, w1_words, w1_scales, w2, w3, gain, w4_words, w4_scales, w5, out
):
    nc = tc.nc
    with ExitStack() as ctx:
        keep = ctx.enter_context(tc.tile_pool(name="keep", bufs=1))
        psum = ctx.enter_context(tc.psum_pool(name="psum", bufs=1))

        def kept(shape, dtype, name, tag=None):
            return keep.tile(shape, dtype, name=name, tag=tag or name, align_bytes=64)

        lists = [keep.tile([P, S // LIST_GROUP], U16, name=f"list{u}") for u in (HELPER, REQUEST, DISTRICT)]
        tab_w = [kept([P, T], I32, f"tab_w{a}") for a in range(PASSES)]
        tab_s = kept([P, T], U8, "tab_s")
        w1_w = kept([P, PASSES, 2 * H], U8, "w1_w")
        w1_s = kept([P, PASSES, H], U8, "w1_s")
        w4_w = kept([P, N], I32, "w4_w")
        w4_s = kept([P, N], U8, "w4_s")
        moved_s = kept([P, S], U8, "moved_s")
        gains = kept([P, PACK], F32, "gains")
        ident = kept([P, P], F32, "ident")
        one = kept([P, 1], F32, "one")
        quarter_pi = kept([P, 1], F32, "quarter_pi")

        nc.vector.memset(tab_s[:].bitcast(I32), 0)
        nc.vector.memset(one[:], 1.0)
        nc.vector.tensor_scalar(out=quarter_pi[:], in0=one[:], scalar1=math.pi / 4.0, scalar2=None, op0=ALU.mult)
        nc.gpsimd.memset(w1_s[:].rearrange("p a c -> p (a c)").bitcast(I32), 0)
        nc.gpsimd.memset(moved_s[:].bitcast(I32), 0)
        nc.gpsimd.memset(w4_s[:].bitcast(I32), 0)

        def load_rows(w, a, c0, c1, name):
            raw = kept([P, PACK, c1 - c0], F32, name)
            rows = w[a * K_PASS : (a + 1) * K_PASS, c0:c1]
            nc.sync.dma_start(out=raw[:], in_=rows.rearrange("(p i) c -> p i c", i=PACK))
            return raw

        def load_table(a):
            nc.sync.dma_start(out=tab_w[a][:], in_=tab_words[a].rearrange("p t i -> p (t i)").bitcast(I32))

        for list_tile, list_input in zip(lists, (offs, offs2, offs3)):
            nc.sync.dma_start(list_tile[:], list_input)
        for quad in range(QUADS):
            nc.sync.dma_start(
                out=tab_s[QUAD * quad : QUAD * quad + ROWS * PASSES, :].bitcast(I32),
                in_=tab_scales[:, ROWS * quad : ROWS * (quad + 1), :].bitcast(I32),
            )
        load_table(0)
        for quad in range(QUADS):
            nc.sync.dma_start(
                out=w1_s[QUAD * quad : QUAD * quad + ROWS, :, :].bitcast(I32),
                in_=w1_scales[:, ROWS * quad : ROWS * (quad + 1), :].rearrange("a s c -> s a c").bitcast(I32),
            )
        nc.sync.dma_start(out=w1_w[:].bitcast(I32), in_=w1_words.rearrange("a p c -> p a c").bitcast(I32))
        load_table(1)
        w2_raw = [load_rows(w2, a, 0, H, f"w2_raw{a}") for a in range(PASSES)]
        w3_raw = [load_rows(w3, a, 0, H, f"w3_raw{a}") for a in range(PASSES)]
        nc.sync.dma_start(out=gains[:], in_=gain.rearrange("(p i) -> p i", i=PACK))
        w5_raw0 = load_rows(w5, 0, 0, N, "w5_raw0")
        w5_raw1a = load_rows(w5, 1, 0, 2 * PART, "w5_raw1a")
        w5_raw1b = load_rows(w5, 1, 2 * PART, N, "w5_raw1b")
        for quad in range(QUADS):
            nc.sync.dma_start(
                out=w4_s[QUAD * quad : QUAD * quad + ROWS, :].bitcast(I32),
                in_=w4_scales[0, ROWS * quad : ROWS * (quad + 1), :].bitcast(I32),
            )
        nc.sync.dma_start(out=w4_w[:], in_=w4_words[0].rearrange("p c i -> p (c i)").bitcast(I32))
        make_identity(nc, ident[:])

        got_s = [kept([P, S], U8, f"got_s{u}") for u in (HELPER, REQUEST, DISTRICT)]
        got_w = [[None] * PASSES for u in (HELPER, REQUEST, DISTRICT)]

        def gather_words(u, a, tag=None):
            got_w[u][a] = kept([P, S], U32, f"got_w{u}{a}", tag)
            nc.vector.tensor_copy(got_w[u][a][:], tab_w[a][:].bitcast(U32).indirect(lists[u][:]))

        for u in (HELPER, REQUEST, DISTRICT):
            nc.vector.tensor_copy(got_s[u][:], tab_s[:].indirect(lists[u][:]))
        nc.scalar.dma_start(
            out=moved_s[0:PLANE_SPAN, :].bitcast(I32), in_=got_s[HELPER][ROWS : ROWS + PLANE_SPAN, :].bitcast(I32)
        )
        for u in (HELPER, REQUEST, DISTRICT):
            gather_words(u, 0)
        gather_words(HELPER, 1)
        gather_words(REQUEST, 1)

        def round_part(copy, raw, c0, name, tag=None):
            grouped = kept([P, PART, PACK], BF16, name, tag)
            copy(
                out=grouped[:].rearrange("p (c e) i -> p c i e", e=RUN),
                in_=raw[:, :, c0 : c0 + PART].rearrange("p i (c e) -> p c i e", e=RUN),
            )
            return grouped

        def quantise(grouped, operand, c0):
            width = grouped.shape[1]
            nc.vector.quantize_mx(
                out=operand[0][:, c0 : c0 + width].bitcast(FP8X4),
                scales=operand[1][:, c0 : c0 + width],
                in_=grouped[:].rearrange("p c i -> p (c i)"),
            )

        def new_operand(width, name):
            return kept([P, width], U32, name + "_w"), kept([P, width], U8, name + "_s")

        def two_parts_on_vector(raw, operand, name):
            groups = [round_part(nc.vector.tensor_copy, raw, g * PART, f"{name}_{g}") for g in range(2)]
            for g, grouped in enumerate(groups):
                quantise(grouped, operand, g * PART)

        def first_product(u, planes, moving, half):
            banks = [psum.tile([P, H], F32, name="bank", tag=f"{half}{jt}") for jt in range(J_TILES)]
            for a in range(PASSES):
                for jt in range(J_TILES):
                    cols = slice(jt * P, (jt + 1) * P)
                    nc.tensor.matmul_mx(
                        out=banks[jt][:],
                        lhsT=got_w[u][a][:, cols].bitcast(FP8X4),
                        lhsT_scale=planes[a][:, cols],
                        rhs=moving[a][0],
                        rhs_scale=moving[a][1],
                        start=(a == 0),
                        stop=(a == PASSES - 1),
                    )
            return [bank[:].rearrange("j (p i) -> j i p", i=PACK) for bank in banks]

        def add_turned(jt, term, first, last):
            for i in range(PACK):
                nc.tensor.matmul(
                    out=sums[jt][:, i, :],
                    lhsT=term[:, i, :],
                    rhs=ident[:],
                    is_transpose=True,
                    start=(first and i == 0),
                    stop=(last and i == PACK - 1),
                )

        def through(func, sources, name, **how):
            terms = [kept([P, PACK, P], F32, f"{name}{jt}") for jt in range(J_TILES)]
            for term, source in zip(terms, sources):
                nc.scalar.activation(out=term[:], in_=source, func=func, **how)
            return terms

        def planes_of(u):
            return [got_s[u][ROWS * a : P, :] for a in range(PASSES)]

        def moving_of(operands):
            return [(words[:].bitcast(FP8X4), scales[:]) for words, scales in operands]

        w1_moving = [(w1_w[:, a, :].bitcast(FP4X4), w1_s[:, a, :]) for a in range(PASSES)]
        tanhs = through(ACT.Tanh, first_product(HELPER, [got_s[HELPER], moved_s], w1_moving, "low"), "tanh")

        w2_q = [new_operand(H, f"w2_q{a}") for a in range(PASSES)]
        for a in range(PASSES):
            two_parts_on_vector(w2_raw[a], w2_q[a], f"w2_{a}")

        request = first_product(REQUEST, planes_of(REQUEST), moving_of(w2_q), "high")
        sines = through(ACT.Sin, request, "sine", scale=0.5, bias=quarter_pi[:])
        sums = [psum.tile([P, PACK, P], F32, name="sum", tag=f"high{jt}") for jt in range(J_TILES)]
        for jt in range(J_TILES):
            add_turned(jt, tanhs[jt], True, False)
        squares = through(ACT.Square, [sine[:] for sine in sines], "square", scale=math.sqrt(2.0))

        gather_words(DISTRICT, 1, f"got_w{REQUEST}1")
        w3_q = [new_operand(H, f"w3_q{a}") for a in range(PASSES)]
        for a in range(PASSES):
            two_parts_on_vector(w3_raw[a], w3_q[a], f"w3_{a}")

        sizes = through(ACT.Abs, first_product(DISTRICT, planes_of(DISTRICT), moving_of(w3_q), "low"), "size")
        for jt in range(J_TILES):
            add_turned(jt, squares[jt], False, False)

        w5_q = [new_operand(N, f"w5_q{a}") for a in range(PASSES)]
        two_parts_on_vector(w5_raw0, w5_q[0], "w5_0")

        h_grouped = kept([P, S, PACK], BF16, "h_grouped")
        for jt in range(J_TILES):
            add_turned(jt, sizes[jt], False, True)
            nc.vector.scalar_tensor_tensor(
                out=h_grouped[:, jt * P : (jt + 1) * P, :],
                in0=sums[jt][:].rearrange("p i j -> p j i"),
                scalar=1.0,
                in1=gains[:].unsqueeze(1).to_broadcast([P, P, PACK]),
                op0=ALU.subtract,
                op1=ALU.mult,
            )
        scalar_parts = [
            (w5_raw0, 2 * PART, 0, 2 * PART),
            (w5_raw1a, 0, 1, 0),
            (w5_raw1a, PART, 1, PART),
            (w5_raw1b, 0, 1, 2 * PART),
        ]
        scalar_groups = [
            round_part(nc.scalar.copy, part[0], part[1], f"w5_late{g}", f"size{g}") for g, part in enumerate(scalar_parts)
        ]
        h_q = new_operand(S, "h_q")
        quantise(h_grouped, h_q, 0)
        for grouped, part in zip(scalar_groups, scalar_parts):
            quantise(grouped, w5_q[part[2]], part[3])

        ys = []
        for nt in range(N // P):
            cols = slice(nt * P, (nt + 1) * P)
            y_bank = psum.tile([P, S], F32, name="y_bank", tag=f"low{nt % J_TILES}")
            nc.tensor.matmul_mx(
                out=y_bank[:],
                lhsT=w4_w[:, cols].bitcast(FP8X4),
                lhsT_scale=w4_s[:, cols],
                rhs=h_q[0][:].bitcast(FP8X4),
                rhs_scale=h_q[1][:],
                start=True,
                stop=True,
            )
            y = kept([P, S], F32, f"y{nt}")
            nc.scalar.copy(out=y[:], in_=y_bank[:])
            ys.append(y)
        for nt in range(N // P):
            cols = slice(nt * P, (nt + 1) * P)
            d_bank = psum.tile([P, S], F32, name="d_bank", tag=f"high{nt % J_TILES}")
            for a in range(PASSES):
                nc.tensor.matmul_mx(
                    out=d_bank[:],
                    lhsT=w5_q[a][0][:, cols].bitcast(FP8X4),
                    lhsT_scale=w5_q[a][1][:, cols],
                    rhs=got_w[DISTRICT][a][:].bitcast(FP8X4),
                    rhs_scale=planes_of(DISTRICT)[a],
                    start=(a == 0),
                    stop=(a == PASSES - 1),
                )
            result = kept([P, S], F32, f"result{nt}")
            nc.vector.tensor_tensor(out=result[:], in0=d_bank[:], in1=ys[nt][:], op=ALU.mult)
            nc.sync.dma_start(out=out[cols, :], in_=result[:])
